import numpy as np
import ml_dtypes


def mxq(x, axis, fmt="e4m3"):
    dtype, down = {"e4m3": (ml_dtypes.float8_e4m3fn, 7), "e5m2": (ml_dtypes.float8_e5m2, 14)}[fmt]
    v = np.moveaxis(np.asarray(x, np.float32).astype(ml_dtypes.bfloat16).astype(np.float64), axis, -1)
    blocks = v.reshape(v.shape[:-1] + (-1, 32))
    amax = np.abs(blocks).max(-1, keepdims=True)
    byte = np.maximum(np.where(amax > 0, np.frexp(amax)[1] - 1 + 127, 0) - down, 1)
    scale = np.exp2(byte - 127.0)
    codes = (blocks / scale).astype(np.float32).astype(dtype).astype(np.float64)
    return np.moveaxis((codes * scale).reshape(v.shape), -1, axis)


WIDE = False


def mx_kscale(k):
    if not WIDE:
        return np.ones(k)
    levels = np.array([10, -10, 5, -5, 0])
    if k % 512:
        return np.exp2(np.random.permutation(np.resize(levels, k // 32))).repeat(32)
    a = np.empty((k // 512, 16))
    for p in range(k // 512):
        a[p, :8] = np.random.permutation(np.resize(levels, 8))
        for g in range(8):
            far = levels[np.abs(levels - a[p, g]) >= 10]
            a[p, g + 8] = far[np.random.randint(len(far))]
    return np.exp2(a.ravel()).repeat(32)


def f64(x):
    return np.asarray(x).astype(np.float64)


def striped8(idx):
    return np.concatenate([x.reshape(-1, 16).T for x in idx]).astype(np.uint16)


def runs(offs, k):
    lists = np.stack([offs[16 * r : 16 * r + 16].T.reshape(-1) for r in range(8)]).astype(np.int64)
    return lists[np.arange(k) % 512 // 64]


def pack_weight(w):
    k, n = w.shape
    w = f64(np.asarray(w, np.float32).astype(ml_dtypes.bfloat16)).reshape(k // 32, 32, n)
    amax = np.abs(w).max(1)
    byte = np.clip(np.where(amax > 0, np.frexp(amax)[1] - 1 + 127 - 7, 1), 1, 254)
    scaled = (w * np.exp2(127.0 - byte)[:, None, :]).reshape(k, n).astype(np.float32)
    words = np.ascontiguousarray(scaled.reshape(k // 512, 128, 4, n).transpose(0, 1, 3, 2)).astype(ml_dtypes.float8_e4m3fn).view(np.uint8)
    return words, np.ascontiguousarray(byte.astype(np.uint8).reshape(k // 512, 16, n))


def unpack_weight(words, scales):
    g, p, n, _ = words.shape
    vals = np.ascontiguousarray(words).view(ml_dtypes.float8_e4m3fn).astype(np.float64) * np.repeat(np.exp2(scales.astype(np.float64) - 127.0), 8, axis=1)[..., None]
    return vals.transpose(0, 1, 3, 2).reshape(g * 512, n)


K, T, S, N, W = 512, 2048, 512, 512, 256


def setup_inputs():
    n = np.random.standard_normal
    s = mx_kscale(K)[:, None]
    packed_xT = pack_weight(n((K, T)) * s)
    perm = np.stack([np.random.permutation(S) for _ in range(8)])
    return {
        "x_words": packed_xT[0],
        "x_scales": packed_xT[1],
        "w1": (n((K, N)) / np.sqrt(2 * K) / s).astype(np.float32),
        "w2": (n((K, N)) / np.sqrt(2 * K) / s).astype(np.float32),
        "offs": striped8(np.random.randint(0, T, (8, S))),
        "hz": striped8(np.random.randint(0, T, (8, S))),
        "n1": striped8(perm[:, :W]),
        "n2": striped8(perm[:, W:]),
    }


def reference(x_words, x_scales, w1, w2, offs, hz, n1, n2):
    xq = unpack_weight(x_words, x_scales)[np.arange(K)[:, None], runs(offs, K)]
    x_hz = unpack_weight(x_words, x_scales)[np.arange(K)[:, None], runs(hz, K)]
    h = mxq(f64(w1), 0, "e4m3").T @ xq + mxq(f64(w2), 0, "e4m3").T @ x_hz
    pa = h[np.arange(N)[:, None], runs(n1, N)]
    pb = h[np.arange(N)[:, None], runs(n2, N)]
    rb = np.maximum(pa, pb)
    ra = pa / (np.abs(pb) + 0.5)
    ds = np.zeros((N, S))
    ds[np.arange(N)[:, None], runs(n1, N)] = ra
    out = ds.copy()
    out[np.arange(N)[:, None], runs(n2, N)] = rb
    return out

@@ -1,0 +1,171 @@
+from contextlib import ExitStack
+
+import concourse.mybir as mybir
+
+K, T, S, N, W = 512, 2048, 512, 512, 256
+FLOPS = 2 * 2 * K * N * S
+
+F32 = mybir.dt.float32
+BF16 = mybir.dt.bfloat16
+U32 = mybir.dt.uint32
+I32 = mybir.dt.int32
+U16 = mybir.dt.uint16
+U8 = mybir.dt.uint8
+FP8X4 = mybir.dt.float8_e4m3fn_x4
+ACT = mybir.ActivationFunctionType
+ALU = mybir.AluOpType
+
+P = 128
+PACK = 4
+TILES = 4
+LINE = 4
+
+
+def tile_picked_ohhratio_none_p_kernel(tc, x_words, x_scales, w1, w2, offs, hz, n1, n2, out):
+    nc = tc.nc
+    with ExitStack() as ctx:
+        keep = ctx.enter_context(tc.tile_pool(name="keep", bufs=1))
+        psum = ctx.enter_context(tc.psum_pool(name="psum", bufs=1))
+
+        offs_t = keep.tile([P, S // 16], U16, name="offs_t")
+        hz_t = keep.tile([P, S // 16], U16, name="hz_t")
+        n1_t = keep.tile([P, W // 16], U16, name="n1_t")
+        n2_t = keep.tile([P, W // 16], U16, name="n2_t")
+        table_words = keep.tile([P, T], U32, name="table_words", align_bytes=64)
+        table_scales = keep.tile([P, T], U8, name="table_scales", tag="scales_then_w2", align_bytes=64)
+        w1_raw = keep.tile([P, PACK, N], F32, name="w1_raw", align_bytes=64)
+        w2_low = keep.tile([P, 2, N], F32, name="w2_low", align_bytes=64)
+        picked_scales = keep.tile([P, 2 * S], U8, name="picked_scales", align_bytes=64)
+        x_planes = keep.tile([P, 2 * S], U8, name="x_planes", align_bytes=64)
+        x_codes = [keep.tile([P, S], U32, name="x_codes%d" % a, align_bytes=64) for a in range(2)]
+        w2_rows = w2.rearrange("(p j) c -> p j c", j=PACK)
+
+        nc.vector.memset(table_scales[:].bitcast(I32), 0)
+        nc.gpsimd.memset(x_planes[:].bitcast(I32), 0)
+        w1_rows = w1.rearrange("(p j) c -> p j c", j=PACK)
+        nc.sync.dma_start(out=w1_raw[:, 0:1, :], in_=w1_rows[:, 0:1, :])
+        nc.sync.dma_start(offs_t[:], offs)
+        nc.sync.dma_start(hz_t[:], hz)
+        nc.sync.dma_start(out=table_scales[0:P:8, :].bitcast(I32), in_=x_scales[0].bitcast(I32))
+        nc.sync.dma_start(out=table_words[:].bitcast(I32), in_=x_words[0].rearrange("p n t -> p (n t)").bitcast(I32))
+        nc.sync.dma_start(n1_t[:], n1)
+        nc.sync.dma_start(n2_t[:], n2)
+        nc.sync.dma_start(out=w1_raw[:, 1:PACK, :], in_=w1_rows[:, 1:PACK, :])
+        nc.sync.dma_start(out=w2_low[:], in_=w2_rows[:, 0:2, :])
+
+        for a, picks in enumerate((offs_t, hz_t)):
+            nc.vector.tensor_copy(picked_scales[:, a * S:(a + 1) * S], table_scales[:].indirect(picks[:]))
+        for i in range(4):
+            nc.sync.dma_start(out=x_planes[i:P:32, :].bitcast(I32), in_=picked_scales[8 * i:P:32, :].bitcast(I32))
+        w2_high = keep.tile([P, 2, N], F32, name="w2_high", tag="scales_then_w2", align_bytes=64)
+        nc.sync.dma_start(out=w2_high[:], in_=w2_rows[:, 2:4, :])
+        for a, picks in enumerate((offs_t, hz_t)):
+            nc.vector.tensor_copy(x_codes[a][:], table_words[:].indirect(picks[:]))
+
+        rounded = [keep.tile([P, 2, P * PACK], BF16, name="rounded%d" % t, align_bytes=64) for t in range(TILES)]
+        w_codes = [keep.tile([P, 2 * P], U32, name="w_codes%d" % t, align_bytes=64) for t in range(TILES)]
+        w_scales = [keep.tile([P, 2 * P], U8, name="w_scales%d" % t, align_bytes=64) for t in range(TILES)]
+
+        def round_rows(copy, a, t, raw, first):
+            rows = raw.shape[1]
+            copy(
+                out=rounded[t][:, a, :].rearrange("p (u i j) -> p u j i", i=LINE, j=PACK)[:, :, first:first + rows, :],
+                in_=raw[:].rearrange("p j (u t i) -> p t u j i", t=TILES, i=LINE)[:, t],
+            )
+
+        def quantise(t, first, last):
+            cols = slice(first * P, last * P)
+            nc.vector.quantize_mx(
+                out=w_codes[t][:, cols].bitcast(FP8X4),
+                scales=w_scales[t][:, cols],
+                in_=rounded[t][:, first:last, :].rearrange("p a c -> p (a c)"),
+            )
+
+        banks = {t: [psum.tile([P, S], F32, name="acc%d" % t)] for t in range(1, TILES)}
+        banks[0] = [psum.tile([P, S // 2], F32, name="acc0_%d" % half) for half in range(2)]
+
+        def product(a, t):
+            width = S // len(banks[t])
+            for b, bank in enumerate(banks[t]):
+                nc.tensor.matmul_mx(
+                    out=bank[:],
+                    lhsT=w_codes[t][:, a * P:(a + 1) * P].bitcast(FP8X4),
+                    lhsT_scale=w_scales[t][:, a * P:(a + 1) * P],
+                    rhs=x_codes[a][:, b * width:(b + 1) * width].bitcast(FP8X4),
+                    rhs_scale=x_planes[:, a * S + b * width:a * S + (b + 1) * width],
+                    start=(a == 0),
+                    stop=(a == 1),
+                )
+
+
+        out_rows = out.rearrange("(u t i) c -> t u (i c)", t=TILES, i=LINE)
+        h = {0: keep.tile([P, S], F32, name="h0", tag="h01")}
+        pa = [keep.tile([P, W], F32, name="pa%d" % t) for t in range(TILES)]
+        pb = [keep.tile([P, W], F32, name="pb%d" % t) for t in range(TILES)]
+        size = [keep.tile([P, W], F32, name="size%d" % t) for t in range(TILES)]
+        root = [keep.tile([P, W], F32, name="root%d" % t, tag="root%d" % t) for t in range(TILES)]
+        inv = [keep.tile([P, W], F32, name="inv%d" % t) for t in range(TILES)]
+        rb = [keep.tile([P, W], F32, name="rb%d" % t) for t in range(TILES)]
+        placed = {}
+
+        def leave_psum(t):
+            h[t] = keep.tile([P, S], F32, name="h%d" % t, tag="h01" if t == 1 else "h%d" % t)
+            nc.scalar.copy(out=h[t][:], in_=banks[t][0][:])
+
+        def fetch(pairs, picks, t):
+            nc.scalar.activation(out=pairs[t][:], in_=h[t][:].indirect(picks[:]), func=ACT.Copy)
+
+        def magnitude(t):
+            nc.scalar.activation(out=size[t][:], in_=pb[t][:], func=ACT.Abs)
+
+        def inverse_root(t):
+            nc.scalar.activation(out=root[t][:], in_=size[t][:], func=ACT.Abs_reciprocal_sqrt, bias=0.5)
+
+        def square(t):
+            nc.scalar.activation(out=inv[t][:], in_=root[t][:], func=ACT.Square)
+
+        def larger(t):
+            nc.vector.tensor_tensor(rb[t][:], pa[t][:], pb[t][:], ALU.max)
+
+        def place_larger(t, tag):
+            placed[t] = keep.tile([P, S], F32, name="placed%d" % t, tag=tag)
+            nc.vector.tensor_copy(placed[t][:].indirect(n2_t[:]), rb[t][:])
+
+        def place_ratio(t):
+            nc.vector.tensor_tensor(placed[t][:].indirect(n1_t[:]), pa[t][:], inv[t][:], ALU.mult)
+            nc.sync.dma_start(out=out_rows[t], in_=placed[t][:])
+
+        for t in range(TILES):
+            round_rows(nc.scalar.copy if t < 2 else nc.vector.tensor_copy, 0, t, w1_raw, 0)
+        quantise(0, 0, 1)
+        product(0, 0)
+        for t in range(TILES):
+            round_rows(nc.scalar.copy if t < 2 else nc.vector.tensor_copy, 1, t, w2_low, 0)
+        round_rows(nc.vector.tensor_copy, 1, 0, w2_high, 2)
+        quantise(0, 1, 2)
+        product(1, 0)
+        nc.scalar.copy(out=h[0][:, 0:S // 2], in_=banks[0][0][:])
+        nc.vector.tensor_copy(out=h[0][:, S // 2:S], in_=banks[0][1][:])
+        fetch(pa, n1_t, 0)
+        nc.vector.tensor_copy(pb[0][:], h[0][:].indirect(n2_t[:]))
+        larger(0)
+        place_larger(0, "placed0")
+        for t in range(1, TILES):
+            round_rows(nc.scalar.copy if t < 3 else nc.vector.tensor_copy, 1, t, w2_high, 2)
+            quantise(t, 0, 2)
+            product(0, t)
+            product(1, t)
+        for t in range(TILES - 1):
+            leave_psum(t + 1)
+            magnitude(t)
+            fetch(pa, n1_t, t + 1)
+            inverse_root(t)
+            fetch(pb, n2_t, t + 1)
+            square(t)
+            larger(t + 1)
+            place_ratio(t)
+            place_larger(t + 1, "root%d" % t)
+        magnitude(3)
+        inverse_root(3)
+        square(3)
+        place_ratio(3)

@@ -42,6 +42,9 @@ def tile_picked_ohhratio_none_p_kernel(tc, x_words, x_scales, w1, w2, offs, hz, 
 
         nc.vector.memset(table_scales[:].bitcast(I32), 0)
         nc.gpsimd.memset(x_planes[:].bitcast(I32), 0)
+        warm = keep.tile([P, 2], F32, name="warm")
+        nc.vector.memset(warm[:, 0:1], 1.0)
+        nc.scalar.activation(out=warm[:, 1:2], in_=warm[:, 0:1], func=ACT.Abs_reciprocal_sqrt)
         w1_rows = w1.rearrange("(p j) c -> p j c", j=PACK)
         nc.sync.dma_start(out=w1_raw[:, 0:1, :], in_=w1_rows[:, 0:1, :])
         nc.sync.dma_start(offs_t[:], offs)

@@ -50,10 +50,10 @@ def tile_picked_ohhratio_none_p_kernel(tc, x_words, x_scales, w1, w2, offs, hz, 
         nc.sync.dma_start(offs_t[:], offs)
         nc.sync.dma_start(hz_t[:], hz)
         nc.sync.dma_start(out=table_scales[0:P:8, :].bitcast(I32), in_=x_scales[0].bitcast(I32))
-        nc.sync.dma_start(out=table_words[:].bitcast(I32), in_=x_words[0].rearrange("p n t -> p (n t)").bitcast(I32))
+        nc.sync.dma_start(out=w1_raw[:, 1:PACK, :], in_=w1_rows[:, 1:PACK, :])
         nc.sync.dma_start(n1_t[:], n1)
         nc.sync.dma_start(n2_t[:], n2)
-        nc.sync.dma_start(out=w1_raw[:, 1:PACK, :], in_=w1_rows[:, 1:PACK, :])
+        nc.sync.dma_start(out=table_words[:].bitcast(I32), in_=x_words[0].rearrange("p n t -> p (n t)").bitcast(I32))
         nc.sync.dma_start(out=w2_low[:], in_=w2_rows[:, 0:2, :])
 
         for a, picks in enumerate((offs_t, hz_t)):
@@ -84,8 +84,8 @@ def tile_picked_ohhratio_none_p_kernel(tc, x_words, x_scales, w1, w2, offs, hz, 
                 in_=rounded[t][:, first:last, :].rearrange("p a c -> p (a c)"),
             )
 
-        banks = {t: [psum.tile([P, S], F32, name="acc%d" % t)] for t in range(1, TILES)}
-        banks[0] = [psum.tile([P, S // 2], F32, name="acc0_%d" % half) for half in range(2)]
+        banks = {t: [psum.tile([P, S], F32, name="acc%d" % t)] for t in range(1, 2)}
+        banks[0] = [psum.tile([P, S // 2], F32, name="acc0_%d" % half, tag="acc0_%d" % half) for half in range(2)]
 
         def product(a, t):
             width = S // len(banks[t])
@@ -112,7 +112,7 @@ def tile_picked_ohhratio_none_p_kernel(tc, x_words, x_scales, w1, w2, offs, hz, 
         placed = {}
 
         def leave_psum(t):
-            h[t] = keep.tile([P, S], F32, name="h%d" % t, tag="h01" if t == 1 else "h%d" % t)
+            h[t] = keep.tile([P, S], F32, name="h%d" % t, tag="h01")
             nc.scalar.copy(out=h[t][:], in_=banks[t][0][:])
 
         def fetch(pairs, picks, t):
@@ -139,36 +139,57 @@ def tile_picked_ohhratio_none_p_kernel(tc, x_words, x_scales, w1, w2, offs, hz, 
             nc.sync.dma_start(out=out_rows[t], in_=placed[t][:])
 
         for t in range(TILES):
-            round_rows(nc.scalar.copy if t < 2 else nc.vector.tensor_copy, 0, t, w1_raw, 0)
-        quantise(0, 0, 1)
+            round_rows(nc.scalar.copy if t else nc.vector.tensor_copy, 0, t, w1_raw, 0)
+        for t in range(2):
+            quantise(t, 0, 1)
         product(0, 0)
+        product(0, 1)
         for t in range(TILES):
-            round_rows(nc.scalar.copy if t < 2 else nc.vector.tensor_copy, 1, t, w2_low, 0)
+            round_rows(nc.scalar.copy, 1, t, w2_low, 0)
         round_rows(nc.vector.tensor_copy, 1, 0, w2_high, 2)
         quantise(0, 1, 2)
         product(1, 0)
-        nc.scalar.copy(out=h[0][:, 0:S // 2], in_=banks[0][0][:])
-        nc.vector.tensor_copy(out=h[0][:, S // 2:S], in_=banks[0][1][:])
+        nc.vector.tensor_copy(out=h[0][:, 0:S // 2], in_=banks[0][0][:])
+        nc.scalar.copy(out=h[0][:, S // 2:S], in_=banks[0][1][:])
         fetch(pa, n1_t, 0)
         nc.vector.tensor_copy(pb[0][:], h[0][:].indirect(n2_t[:]))
         larger(0)
+        nc.vector.scalar_tensor_tensor(out=size[0][:], in0=pb[0][:], scalar=-1.0, in1=pb[0][:], op0=ALU.mult, op1=ALU.max)
         place_larger(0, "placed0")
         for t in range(1, TILES):
-            round_rows(nc.scalar.copy if t < 3 else nc.vector.tensor_copy, 1, t, w2_high, 2)
-            quantise(t, 0, 2)
+            round_rows(nc.scalar.copy if t == 1 else nc.vector.tensor_copy, 1, t, w2_high, 2)
+            quantise(t, 1 if t == 1 else 0, 2)
+        product(1, 1)
+        for t in range(2, TILES):
+            banks[t] = [psum.tile([P, S], F32, name="acc%d" % t, tag="acc0_%d" % (t - 2))]
             product(0, t)
             product(1, t)
-        for t in range(TILES - 1):
-            leave_psum(t + 1)
-            magnitude(t)
-            fetch(pa, n1_t, t + 1)
+        leave_psum(1)
+        fetch(pa, n1_t, 1)
+        fetch(pb, n2_t, 1)
+        inverse_root(0)
+        square(0)
+        larger(1)
+        place_ratio(0)
+        place_larger(1, "root0")
+        leave_psum(2)
+        magnitude(1)
+        fetch(pa, n1_t, 2)
+        inverse_root(1)
+        fetch(pb, n2_t, 2)
+        square(1)
+        larger(2)
+        place_ratio(1)
+        leave_psum(3)
+        magnitude(2)
+        fetch(pa, n1_t, 3)
+        fetch(pb, n2_t, 3)
+        larger(3)
+        place_larger(2, "h01")
+        place_larger(3, "placed3")
+        for t in (2, 3):
+            if t == 3:
+                magnitude(t)
             inverse_root(t)
-            fetch(pb, n2_t, t + 1)
             square(t)
-            larger(t + 1)
             place_ratio(t)
-            place_larger(t + 1, "root%d" % t)
-        magnitude(3)
-        inverse_root(3)
-        square(3)
-        place_ratio(3)

from contextlib import ExitStack

import concourse.mybir as mybir

K, T, S, N, W = 512, 2048, 512, 512, 256
FLOPS = 2 * 2 * K * N * S

F32 = mybir.dt.float32
BF16 = mybir.dt.bfloat16
U32 = mybir.dt.uint32
I32 = mybir.dt.int32
U16 = mybir.dt.uint16
U8 = mybir.dt.uint8
FP8X4 = mybir.dt.float8_e4m3fn_x4
ACT = mybir.ActivationFunctionType
ALU = mybir.AluOpType

P = 128
PACK = 4
TILES = 4
LINE = 4


def tile_picked_ohhratio_none_p_kernel(tc, x_words, x_scales, w1, w2, offs, hz, n1, n2, out):
    nc = tc.nc
    with ExitStack() as ctx:
        keep = ctx.enter_context(tc.tile_pool(name="keep", bufs=1))
        psum = ctx.enter_context(tc.psum_pool(name="psum", bufs=1))

        offs_t = keep.tile([P, S // 16], U16, name="offs_t")
        hz_t = keep.tile([P, S // 16], U16, name="hz_t")
        n1_t = keep.tile([P, W // 16], U16, name="n1_t")
        n2_t = keep.tile([P, W // 16], U16, name="n2_t")
        table_words = keep.tile([P, T], U32, name="table_words", align_bytes=64)
        table_scales = keep.tile([P, T], U8, name="table_scales", tag="scales_then_w2", align_bytes=64)
        w1_raw = keep.tile([P, PACK, N], F32, name="w1_raw", align_bytes=64)
        w2_low = keep.tile([P, 2, N], F32, name="w2_low", align_bytes=64)
        picked_scales = keep.tile([P, 2 * S], U8, name="picked_scales", align_bytes=64)
        x_planes = keep.tile([P, 2 * S], U8, name="x_planes", align_bytes=64)
        x_codes = [keep.tile([P, S], U32, name="x_codes%d" % a, align_bytes=64) for a in range(2)]
        w2_rows = w2.rearrange("(p j) c -> p j c", j=PACK)

        nc.vector.memset(table_scales[:].bitcast(I32), 0)
        nc.gpsimd.memset(x_planes[:].bitcast(I32), 0)
        warm = keep.tile([P, 2], F32, name="warm")
        nc.vector.memset(warm[:, 0:1], 1.0)
        nc.scalar.activation(out=warm[:, 1:2], in_=warm[:, 0:1], func=ACT.Abs_reciprocal_sqrt)
        w1_rows = w1.rearrange("(p j) c -> p j c", j=PACK)
        nc.sync.dma_start(out=w1_raw[:, 0:1, :], in_=w1_rows[:, 0:1, :])
        nc.sync.dma_start(offs_t[:], offs)
        nc.sync.dma_start(hz_t[:], hz)
        nc.sync.dma_start(out=table_scales[0:P:8, :].bitcast(I32), in_=x_scales[0].bitcast(I32))
        nc.sync.dma_start(out=w1_raw[:, 1:PACK, :], in_=w1_rows[:, 1:PACK, :])
        nc.sync.dma_start(n1_t[:], n1)
        nc.sync.dma_start(n2_t[:], n2)
        nc.sync.dma_start(out=table_words[:].bitcast(I32), in_=x_words[0].rearrange("p n t -> p (n t)").bitcast(I32))
        nc.sync.dma_start(out=w2_low[:], in_=w2_rows[:, 0:2, :])

        for a, picks in enumerate((offs_t, hz_t)):
            nc.vector.tensor_copy(picked_scales[:, a * S:(a + 1) * S], table_scales[:].indirect(picks[:]))
        for i in range(4):
            nc.sync.dma_start(out=x_planes[i:P:32, :].bitcast(I32), in_=picked_scales[8 * i:P:32, :].bitcast(I32))
        w2_high = keep.tile([P, 2, N], F32, name="w2_high", tag="scales_then_w2", align_bytes=64)
        nc.sync.dma_start(out=w2_high[:], in_=w2_rows[:, 2:4, :])
        for a, picks in enumerate((offs_t, hz_t)):
            nc.vector.tensor_copy(x_codes[a][:], table_words[:].indirect(picks[:]))

        rounded = [keep.tile([P, 2, P * PACK], BF16, name="rounded%d" % t, align_bytes=64) for t in range(TILES)]
        w_codes = [keep.tile([P, 2 * P], U32, name="w_codes%d" % t, align_bytes=64) for t in range(TILES)]
        w_scales = [keep.tile([P, 2 * P], U8, name="w_scales%d" % t, align_bytes=64) for t in range(TILES)]

        def round_rows(copy, a, t, raw, first):
            rows = raw.shape[1]
            copy(
                out=rounded[t][:, a, :].rearrange("p (u i j) -> p u j i", i=LINE, j=PACK)[:, :, first:first + rows, :],
                in_=raw[:].rearrange("p j (u t i) -> p t u j i", t=TILES, i=LINE)[:, t],
            )

        def quantise(t, first, last):
            cols = slice(first * P, last * P)
            nc.vector.quantize_mx(
                out=w_codes[t][:, cols].bitcast(FP8X4),
                scales=w_scales[t][:, cols],
                in_=rounded[t][:, first:last, :].rearrange("p a c -> p (a c)"),
            )

        banks = {t: [psum.tile([P, S], F32, name="acc%d" % t)] for t in range(1, 2)}
        banks[0] = [psum.tile([P, S // 2], F32, name="acc0_%d" % half, tag="acc0_%d" % half) for half in range(2)]

        def product(a, t):
            width = S // len(banks[t])
            for b, bank in enumerate(banks[t]):
                nc.tensor.matmul_mx(
                    out=bank[:],
                    lhsT=w_codes[t][:, a * P:(a + 1) * P].bitcast(FP8X4),
                    lhsT_scale=w_scales[t][:, a * P:(a + 1) * P],
                    rhs=x_codes[a][:, b * width:(b + 1) * width].bitcast(FP8X4),
                    rhs_scale=x_planes[:, a * S + b * width:a * S + (b + 1) * width],
                    start=(a == 0),
                    stop=(a == 1),
                )


        out_rows = out.rearrange("(u t i) c -> t u (i c)", t=TILES, i=LINE)
        h = {0: keep.tile([P, S], F32, name="h0", tag="h01")}
        pa = [keep.tile([P, W], F32, name="pa%d" % t) for t in range(TILES)]
        pb = [keep.tile([P, W], F32, name="pb%d" % t) for t in range(TILES)]
        size = [keep.tile([P, W], F32, name="size%d" % t) for t in range(TILES)]
        root = [keep.tile([P, W], F32, name="root%d" % t, tag="root%d" % t) for t in range(TILES)]
        inv = [keep.tile([P, W], F32, name="inv%d" % t) for t in range(TILES)]
        rb = [keep.tile([P, W], F32, name="rb%d" % t) for t in range(TILES)]
        placed = {}

        def leave_psum(t):
            h[t] = keep.tile([P, S], F32, name="h%d" % t, tag="h01")
            nc.scalar.copy(out=h[t][:], in_=banks[t][0][:])

        def fetch(pairs, picks, t):
            nc.scalar.activation(out=pairs[t][:], in_=h[t][:].indirect(picks[:]), func=ACT.Copy)

        def magnitude(t):
            nc.scalar.activation(out=size[t][:], in_=pb[t][:], func=ACT.Abs)

        def inverse_root(t):
            nc.scalar.activation(out=root[t][:], in_=size[t][:], func=ACT.Abs_reciprocal_sqrt, bias=0.5)

        def square(t):
            nc.scalar.activation(out=inv[t][:], in_=root[t][:], func=ACT.Square)

        def larger(t):
            nc.vector.tensor_tensor(rb[t][:], pa[t][:], pb[t][:], ALU.max)

        def place_larger(t, tag):
            placed[t] = keep.tile([P, S], F32, name="placed%d" % t, tag=tag)
            nc.vector.tensor_copy(placed[t][:].indirect(n2_t[:]), rb[t][:])

        def place_ratio(t):
            nc.vector.tensor_tensor(placed[t][:].indirect(n1_t[:]), pa[t][:], inv[t][:], ALU.mult)
            nc.sync.dma_start(out=out_rows[t], in_=placed[t][:])

        for t in range(TILES):
            round_rows(nc.scalar.copy if t else nc.vector.tensor_copy, 0, t, w1_raw, 0)
        for t in range(2):
            quantise(t, 0, 1)
        product(0, 0)
        product(0, 1)
        for t in range(TILES):
            round_rows(nc.scalar.copy, 1, t, w2_low, 0)
        round_rows(nc.vector.tensor_copy, 1, 0, w2_high, 2)
        quantise(0, 1, 2)
        product(1, 0)
        nc.vector.tensor_copy(out=h[0][:, 0:S // 2], in_=banks[0][0][:])
        nc.scalar.copy(out=h[0][:, S // 2:S], in_=banks[0][1][:])
        fetch(pa, n1_t, 0)
        nc.vector.tensor_copy(pb[0][:], h[0][:].indirect(n2_t[:]))
        larger(0)
        nc.vector.scalar_tensor_tensor(out=size[0][:], in0=pb[0][:], scalar=-1.0, in1=pb[0][:], op0=ALU.mult, op1=ALU.max)
        place_larger(0, "placed0")
        for t in range(1, TILES):
            round_rows(nc.scalar.copy if t == 1 else nc.vector.tensor_copy, 1, t, w2_high, 2)
            quantise(t, 1 if t == 1 else 0, 2)
        product(1, 1)
        for t in range(2, TILES):
            banks[t] = [psum.tile([P, S], F32, name="acc%d" % t, tag="acc0_%d" % (t - 2))]
            product(0, t)
            product(1, t)
        leave_psum(1)
        fetch(pa, n1_t, 1)
        fetch(pb, n2_t, 1)
        inverse_root(0)
        square(0)
        larger(1)
        place_ratio(0)
        place_larger(1, "root0")
        leave_psum(2)
        magnitude(1)
        fetch(pa, n1_t, 2)
        inverse_root(1)
        fetch(pb, n2_t, 2)
        square(1)
        larger(2)
        place_ratio(1)
        leave_psum(3)
        magnitude(2)
        fetch(pa, n1_t, 3)
        fetch(pb, n2_t, 3)
        larger(3)
        place_larger(2, "h01")
        place_larger(3, "placed3")
        for t in (2, 3):
            if t == 3:
                magnitude(t)
            inverse_root(t)
            square(t)
            place_ratio(t)
